import numpy as np
import ml_dtypes


def mxq(x, axis, fmt="e4m3"):
    dtype, down = {"e4m3": (ml_dtypes.float8_e4m3fn, 7), "e5m2": (ml_dtypes.float8_e5m2, 14)}[fmt]
    v = np.moveaxis(np.asarray(x, np.float32).astype(ml_dtypes.bfloat16).astype(np.float64), axis, -1)
    blocks = v.reshape(v.shape[:-1] + (-1, 32))
    amax = np.abs(blocks).max(-1, keepdims=True)
    byte = np.maximum(np.where(amax > 0, np.frexp(amax)[1] - 1 + 127, 0) - down, 1)
    scale = np.exp2(byte - 127.0)
    codes = (blocks / scale).astype(np.float32).astype(dtype).astype(np.float64)
    return np.moveaxis((codes * scale).reshape(v.shape), -1, axis)


WIDE = False


def mx_kscale(k):
    if not WIDE:
        return np.ones(k)
    levels = np.array([10, -10, 5, -5, 0])
    if k % 512:
        return np.exp2(np.random.permutation(np.resize(levels, k // 32))).repeat(32)
    a = np.empty((k // 512, 16))
    for p in range(k // 512):
        a[p, :8] = np.random.permutation(np.resize(levels, 8))
        for g in range(8):
            far = levels[np.abs(levels - a[p, g]) >= 10]
            a[p, g + 8] = far[np.random.randint(len(far))]
    return np.exp2(a.ravel()).repeat(32)


def f64(x):
    return np.asarray(x).astype(np.float64)


def striped8(idx):
    return np.asarray(idx).reshape(8, -1, 16).transpose(0, 2, 1).reshape(128, -1).astype(np.uint16)


def unstriped8(offs):
    return offs.reshape(8, 16, -1).transpose(0, 2, 1).reshape(8, -1).astype(np.int64)


def pick8(x, idx, run):
    r = np.arange(len(x))
    return x[r[:, None], idx[r % (8 * run) // run]]


E2M1 = np.array([0.0, 0.5, 1.0, 1.5, 2.0, 3.0, 4.0, 6.0, -0.0, -0.5, -1.0, -1.5, -2.0, -3.0, -4.0, -6.0])


def pack_weight(w, fmt):
    k, n = w.shape
    w = f64(np.asarray(w, np.float32).astype(ml_dtypes.bfloat16)).reshape(k // 32, 32, n)
    amax = np.abs(w).max(1)
    if fmt == "e4m3":
        byte = np.frexp(amax)[1] - 1 + 127 - 7
    else:
        mant, ex = np.frexp(amax / 6.0)
        byte = np.where(mant > 0.5, ex, ex - 1) + 127
    byte = np.clip(np.where(amax > 0, byte, 1), 1, 254)
    scaled = (w * np.exp2(127.0 - byte)[:, None, :]).reshape(k, n).astype(np.float32)
    by_word = np.ascontiguousarray(scaled.reshape(k // 512, 128, 4, n).transpose(0, 1, 3, 2))
    if fmt == "e4m3":
        words = by_word.astype(ml_dtypes.float8_e4m3fn).view(np.uint8)
    else:
        c = by_word.astype(ml_dtypes.float4_e2m1fn).view(np.uint8) & 0xF
        words = (c[..., 0::2] | (c[..., 1::2] << 4)).reshape(k // 512, 128, 2 * n)
    return np.ascontiguousarray(words), np.ascontiguousarray(byte.astype(np.uint8).reshape(k // 512, 16, n))


def unpack_weight(words, scales, fmt):
    g, _, n = scales.shape
    words = np.ascontiguousarray(words).reshape(g, 128, n, -1)
    if fmt == "e4m3":
        vals = words.view(ml_dtypes.float8_e4m3fn).astype(np.float64)
    else:
        nib = np.empty((g, 128, n, 4), np.uint8)
        nib[..., 0::2] = words & 0xF
        nib[..., 1::2] = words >> 4
        vals = E2M1[nib]
    vals = vals * np.repeat(np.exp2(scales.astype(np.float64) - 127.0), 8, axis=1)[..., None]
    return vals.transpose(0, 1, 3, 2).reshape(g * 512, n)


D, T, U, I, Q = 512, 1024, 1024, 512, 128


def setup_inputs():
    n = np.random.standard_normal
    idx = np.stack([np.random.permutation(T)[:I] for _ in range(8)])
    idx2 = np.stack([np.random.permutation(U)[:I] for _ in range(8)])
    idx3 = np.stack([np.random.permutation(T)[:I] for _ in range(8)])
    idx4 = np.stack([np.random.permutation(U)[:I] for _ in range(8)])
    fd = mx_kscale(D)
    keysp = pack_weight(n((D, T)) / fd[:, None], "e2m1")
    notesp = pack_weight(n((D, U)) / fd[:, None], "e4m3")
    return {
        "query": (n((D, Q)) * 1.0 / np.sqrt(D) * fd[:, None]).astype(np.float32),
        "keys_words": keysp[0],
        "keys_scales": keysp[1],
        "notes_words": notesp[0],
        "notes_scales": notesp[1],
        "lam": (np.random.uniform(0.5, 1.5, (Q, 1))).astype(np.float32),
        "offs": striped8(idx),
        "offs2": striped8(idx2),
        "offs3": striped8(idx3),
        "offs4": striped8(idx4),
    }


def reference(query, keys_words, keys_scales, notes_words, notes_scales, lam, offs, offs2, offs3, offs4):
    idx = unstriped8(offs)
    idx2 = unstriped8(offs2)
    idx3 = unstriped8(offs3)
    idx4 = unstriped8(offs4)
    keysu = unpack_weight(keys_words, keys_scales, "e2m1")
    notesu = unpack_weight(notes_words, notes_scales, "e4m3")
    queryq = mxq(f64(query), 0, "e4m3")
    a = queryq.T @ keysu
    b = queryq.T @ notesu
    r = pick8(b, idx2, 16) - pick8(a, idx, 16)
    f1 = np.zeros((Q, T))
    f1[np.arange(Q)[:, None], idx[np.arange(Q) % 128 // 16]] = r
    f2 = np.zeros((Q, U))
    f2[np.arange(Q)[:, None], idx2[np.arange(Q) % 128 // 16]] = r
    a2 = a + f1
    b2 = b - f2
    y = pick8(a2, idx3, 16) - pick8(b2, idx4, 16) * f64(lam)
    return y

@@ -1,0 +1,127 @@
+from contextlib import ExitStack
+
+import concourse.mybir as mybir
+
+D, T, U, I, Q = 512, 1024, 1024, 512, 128
+FLOPS = 2 * D * Q * (T + U)
+
+F32 = mybir.dt.float32
+BF16 = mybir.dt.bfloat16
+I32 = mybir.dt.int32
+U32 = mybir.dt.uint32
+U16 = mybir.dt.uint16
+U8 = mybir.dt.uint8
+FP8X4 = mybir.dt.float8_e4m3fn_x4
+FP4X4 = mybir.dt.float4_e2m1fn_x4
+ADD = mybir.AluOpType.add
+SUB = mybir.AluOpType.subtract
+MULT = mybir.AluOpType.mult
+COPY = mybir.ActivationFunctionType.Copy
+
+P = 128
+PACK = 4
+N = 256
+HALF = I // 2
+SPLIT = 704
+
+
+def tile_attend_traded_two_kernel(tc, query, keys_words, keys_scales, notes_words, notes_scales, lam, offs, offs2, offs3, offs4, out):
+    nc = tc.nc
+    with ExitStack() as ctx:
+        sb = ctx.enter_context(tc.tile_pool(name="sb", bufs=1))
+        ps = ctx.enter_context(tc.psum_pool(name="ps", bufs=1))
+
+        k_scale = sb.tile([P, T], U8, name="k_scale", align_bytes=64)
+        n_scale = sb.tile([P, U], U8, name="n_scale", align_bytes=64)
+        nc.gpsimd.memset(k_scale[:].bitcast(I32), 0)
+        nc.gpsimd.memset(n_scale[:].bitcast(I32), 0)
+
+        q_raw = sb.tile([P, PACK, Q], F32, name="q_raw")
+        nc.sync.dma_start(out=q_raw[:], in_=query.rearrange("(p j) w -> p j w", j=PACK))
+        for r in range(4):
+            nc.sync.dma_start(out=k_scale[32 * r : 32 * r + 4, :].bitcast(I32), in_=keys_scales[0, 4 * r : 4 * r + 4, :].bitcast(I32))
+        k_words = sb.tile([P, 2 * T], U8, name="k_words", align_bytes=64)
+        nc.sync.dma_start(out=k_words[:].bitcast(I32), in_=keys_words[0].bitcast(I32))
+        n_words = sb.tile([P, U], U32, name="n_words", align_bytes=64)
+        nc.sync.dma_start(out=n_words[:].bitcast(I32), in_=notes_words[0].rearrange("p n t -> p (n t)").bitcast(I32))
+        for r in range(4):
+            nc.sync.dma_start(out=n_scale[32 * r : 32 * r + 4, :].bitcast(I32), in_=notes_scales[0, 4 * r : 4 * r + 4, :].bitcast(I32))
+        lists = []
+        for name, src in (("l1", offs), ("l2", offs2), ("l4", offs4), ("l3", offs3)):
+            tile = sb.tile([P, I // 16], U16, name=name)
+            nc.sync.dma_start(tile[:], src)
+            lists.append(tile)
+        l1, l2, l4, l3 = lists
+        lam_col = sb.tile([P, 1], F32, name="lam_col")
+        nc.sync.dma_start(out=lam_col[:], in_=lam)
+
+        f1 = sb.tile([P, T], F32, name="f1")
+        f2 = sb.tile([P, U], F32, name="f2")
+        nc.vector.memset(f2[:], 0.0)
+        nc.vector.memset(f1[:], 0.0)
+
+        q_bf = sb.tile([P, Q, PACK], BF16, name="q_bf", align_bytes=64)
+        nc.vector.tensor_copy(
+            out=q_bf[:].rearrange("p (c i) j -> p c j i", i=4),
+            in_=q_raw[:].rearrange("p j (c i) -> p c j i", i=4),
+        )
+        q_words = sb.tile([P, Q], U32, name="q_words", align_bytes=64)
+        q_scale = sb.tile([P, Q], U8, name="q_scale", align_bytes=64)
+        nc.vector.quantize_mx(out=q_words[:].bitcast(FP8X4), scales=q_scale[:], in_=q_bf[:].rearrange("p w j -> p (w j)"))
+
+        a_ps = [ps.tile([P, N], F32, name="a_ps%d" % c) for c in range(T // N)]
+        b_ps = [ps.tile([P, N], F32, name="b_ps%d" % c) for c in range(U // N)]
+        a = sb.tile([P, T], F32, name="a")
+        b = sb.tile([P, U], F32, name="b")
+        for c in range(T // N):
+            nc.tensor.matmul_mx(
+                out=a_ps[c][:], lhsT=q_words[:].bitcast(FP8X4), lhsT_scale=q_scale[:],
+                rhs=k_words[:, 2 * N * c : 2 * N * (c + 1)].bitcast(FP4X4), rhs_scale=k_scale[:, N * c : N * (c + 1)],
+                start=True, stop=True,
+            )
+            if c % 2 == 0:
+                nc.scalar.copy(out=a[:, N * c : N * (c + 1)], in_=a_ps[c][:])
+            else:
+                nc.vector.tensor_copy(out=a[:, N * c : N * (c + 1)], in_=a_ps[c][:])
+        for c in range(U // N):
+            nc.tensor.matmul_mx(
+                out=b_ps[c][:], lhsT=q_words[:].bitcast(FP8X4), lhsT_scale=q_scale[:],
+                rhs=n_words[:, N * c : N * (c + 1)].bitcast(FP8X4), rhs_scale=n_scale[:, N * c : N * (c + 1)],
+                start=True, stop=True,
+            )
+            nc.vector.tensor_copy(out=b[:, N * c : N * (c + 1)], in_=b_ps[c][:])
+
+        h = [slice(0, HALF // 16), slice(HALF // 16, I // 16)]
+        got_a = [sb.tile([P, HALF], F32, name="got_a%d" % s) for s in range(2)]
+        got_b = sb.tile([P, HALF], F32, name="got_b")
+        r = sb.tile([P, I], F32, name="r")
+        for s in range(2):
+            nc.scalar.activation(got_a[s][:], a[:].indirect(l1[:, h[s]]), COPY)
+        nc.vector.tensor_tensor(r[:, :HALF], b[:].indirect(l2[:, h[0]]), got_a[0][:], SUB)
+        nc.scalar.activation(got_b[:], b[:].indirect(l2[:, h[1]]), COPY)
+        nc.gpsimd.tensor_tensor(r[:, HALF:], got_b[:], got_a[1][:], SUB)
+
+        nc.vector.tensor_copy(f2[:].indirect(l2[:, h[0]]), r[:, :HALF])
+        nc.vector.tensor_copy(f2[:].indirect(l2[:, h[1]]), r[:, HALF:])
+        b2 = sb.tile([P, U], F32, name="b2")
+        nc.gpsimd.tensor_tensor(b2[:], b[:], f2[:], SUB)
+        nc.vector.tensor_copy(f1[:].indirect(l1[:]), r[:])
+        got_b2 = sb.tile([P, HALF], F32, name="got_b2", tag="late")
+        nc.scalar.activation(got_b2[:], b2[:].indirect(l4[:, h[0]]), COPY)
+        lam_b2 = sb.tile([P, HALF], F32, name="lam_b2")
+        nc.scalar.activation(lam_b2[:], got_b2[:], COPY, scale=lam_col[:])
+        neg_b2 = sb.tile([P, HALF], F32, name="neg_b2")
+        nc.scalar.activation(neg_b2[:], b2[:].indirect(l4[:, h[1]]), COPY, scale=-1.0)
+        a2 = sb.tile([P, T], F32, name="a2")
+        nc.gpsimd.tensor_tensor(a2[:, SPLIT:], a[:, SPLIT:], f1[:, SPLIT:], ADD)
+        for c0 in range(0, SPLIT, N):
+            w = min(N, SPLIT - c0)
+            nc.vector.tensor_tensor(a2[:, c0 : c0 + w], a_ps[c0 // N][:, :w], f1[:, c0 : c0 + w], ADD)
+
+        y = [sb.tile([P, HALF], F32, name="y%d" % s) for s in range(2)]
+        got_a2 = sb.tile([P, HALF], F32, name="got_a2", tag="late")
+        nc.scalar.activation(got_a2[:], a2[:].indirect(l3[:, h[1]]), COPY)
+        nc.vector.tensor_tensor(y[0][:], a2[:].indirect(l3[:, h[0]]), lam_b2[:], SUB)
+        nc.sync.dma_start(out=out[:, :HALF], in_=y[0][:])
+        nc.vector.scalar_tensor_tensor(y[1][:], neg_b2[:], lam_col[:], got_a2[:], MULT, ADD)
+        nc.scalar.dma_start(out=out[:, HALF:], in_=y[1][:])

@@ -22,7 +22,8 @@ P = 128
 PACK = 4
 N = 256
 HALF = I // 2
-SPLIT = 704
+SPLIT = 608
+CAST = 48
 
 
 def tile_attend_traded_two_kernel(tc, query, keys_words, keys_scales, notes_words, notes_scales, lam, offs, offs2, offs3, offs4, out):
@@ -33,8 +34,8 @@ def tile_attend_traded_two_kernel(tc, query, keys_words, keys_scales, notes_word
 
         k_scale = sb.tile([P, T], U8, name="k_scale", align_bytes=64)
         n_scale = sb.tile([P, U], U8, name="n_scale", align_bytes=64)
-        nc.gpsimd.memset(k_scale[:].bitcast(I32), 0)
-        nc.gpsimd.memset(n_scale[:].bitcast(I32), 0)
+        nc.vector.memset(k_scale[:].bitcast(I32), 0)
+        nc.vector.memset(n_scale[:].bitcast(I32), 0)
 
         q_raw = sb.tile([P, PACK, Q], F32, name="q_raw")
         nc.sync.dma_start(out=q_raw[:], in_=query.rearrange("(p j) w -> p j w", j=PACK))
@@ -57,13 +58,17 @@ def tile_attend_traded_two_kernel(tc, query, keys_words, keys_scales, notes_word
 
         f1 = sb.tile([P, T], F32, name="f1")
         f2 = sb.tile([P, U], F32, name="f2")
-        nc.vector.memset(f2[:], 0.0)
-        nc.vector.memset(f1[:], 0.0)
+        nc.vector.memset(f2[:].bitcast(I32), 0)
+        nc.vector.memset(f1[:].bitcast(I32), 0)
 
         q_bf = sb.tile([P, Q, PACK], BF16, name="q_bf", align_bytes=64)
+        nc.scalar.copy(
+            out=q_bf[:, CAST:, :].rearrange("p (c i) j -> p c j i", i=4),
+            in_=q_raw[:, :, CAST:].rearrange("p j (c i) -> p c j i", i=4),
+        )
         nc.vector.tensor_copy(
-            out=q_bf[:].rearrange("p (c i) j -> p c j i", i=4),
-            in_=q_raw[:].rearrange("p j (c i) -> p c j i", i=4),
+            out=q_bf[:, :CAST, :].rearrange("p (c i) j -> p c j i", i=4),
+            in_=q_raw[:, :, :CAST].rearrange("p j (c i) -> p c j i", i=4),
         )
         q_words = sb.tile([P, Q], U32, name="q_words", align_bytes=64)
         q_scale = sb.tile([P, Q], U8, name="q_scale", align_bytes=64)
@@ -89,7 +94,10 @@ def tile_attend_traded_two_kernel(tc, query, keys_words, keys_scales, notes_word
                 rhs=n_words[:, N * c : N * (c + 1)].bitcast(FP8X4), rhs_scale=n_scale[:, N * c : N * (c + 1)],
                 start=True, stop=True,
             )
-            nc.vector.tensor_copy(out=b[:, N * c : N * (c + 1)], in_=b_ps[c][:])
+            if c == U // N - 1:
+                nc.scalar.copy(out=b[:, N * c : N * (c + 1)], in_=b_ps[c][:])
+            else:
+                nc.vector.tensor_copy(out=b[:, N * c : N * (c + 1)], in_=b_ps[c][:])
 
         h = [slice(0, HALF // 16), slice(HALF // 16, I // 16)]
         got_a = [sb.tile([P, HALF], F32, name="got_a%d" % s) for s in range(2)]

from contextlib import ExitStack

import concourse.mybir as mybir

D, T, U, I, Q = 512, 1024, 1024, 512, 128
FLOPS = 2 * D * Q * (T + U)

F32 = mybir.dt.float32
BF16 = mybir.dt.bfloat16
I32 = mybir.dt.int32
U32 = mybir.dt.uint32
U16 = mybir.dt.uint16
U8 = mybir.dt.uint8
FP8X4 = mybir.dt.float8_e4m3fn_x4
FP4X4 = mybir.dt.float4_e2m1fn_x4
ADD = mybir.AluOpType.add
SUB = mybir.AluOpType.subtract
MULT = mybir.AluOpType.mult
COPY = mybir.ActivationFunctionType.Copy

P = 128
PACK = 4
N = 256
HALF = I // 2
SPLIT = 608
CAST = 48


def tile_attend_traded_two_kernel(tc, query, keys_words, keys_scales, notes_words, notes_scales, lam, offs, offs2, offs3, offs4, out):
    nc = tc.nc
    with ExitStack() as ctx:
        sb = ctx.enter_context(tc.tile_pool(name="sb", bufs=1))
        ps = ctx.enter_context(tc.psum_pool(name="ps", bufs=1))

        k_scale = sb.tile([P, T], U8, name="k_scale", align_bytes=64)
        n_scale = sb.tile([P, U], U8, name="n_scale", align_bytes=64)
        nc.vector.memset(k_scale[:].bitcast(I32), 0)
        nc.vector.memset(n_scale[:].bitcast(I32), 0)

        q_raw = sb.tile([P, PACK, Q], F32, name="q_raw")
        nc.sync.dma_start(out=q_raw[:], in_=query.rearrange("(p j) w -> p j w", j=PACK))
        for r in range(4):
            nc.sync.dma_start(out=k_scale[32 * r : 32 * r + 4, :].bitcast(I32), in_=keys_scales[0, 4 * r : 4 * r + 4, :].bitcast(I32))
        k_words = sb.tile([P, 2 * T], U8, name="k_words", align_bytes=64)
        nc.sync.dma_start(out=k_words[:].bitcast(I32), in_=keys_words[0].bitcast(I32))
        n_words = sb.tile([P, U], U32, name="n_words", align_bytes=64)
        nc.sync.dma_start(out=n_words[:].bitcast(I32), in_=notes_words[0].rearrange("p n t -> p (n t)").bitcast(I32))
        for r in range(4):
            nc.sync.dma_start(out=n_scale[32 * r : 32 * r + 4, :].bitcast(I32), in_=notes_scales[0, 4 * r : 4 * r + 4, :].bitcast(I32))
        lists = []
        for name, src in (("l1", offs), ("l2", offs2), ("l4", offs4), ("l3", offs3)):
            tile = sb.tile([P, I // 16], U16, name=name)
            nc.sync.dma_start(tile[:], src)
            lists.append(tile)
        l1, l2, l4, l3 = lists
        lam_col = sb.tile([P, 1], F32, name="lam_col")
        nc.sync.dma_start(out=lam_col[:], in_=lam)

        f1 = sb.tile([P, T], F32, name="f1")
        f2 = sb.tile([P, U], F32, name="f2")
        nc.vector.memset(f2[:].bitcast(I32), 0)
        nc.vector.memset(f1[:].bitcast(I32), 0)

        q_bf = sb.tile([P, Q, PACK], BF16, name="q_bf", align_bytes=64)
        nc.scalar.copy(
            out=q_bf[:, CAST:, :].rearrange("p (c i) j -> p c j i", i=4),
            in_=q_raw[:, :, CAST:].rearrange("p j (c i) -> p c j i", i=4),
        )
        nc.vector.tensor_copy(
            out=q_bf[:, :CAST, :].rearrange("p (c i) j -> p c j i", i=4),
            in_=q_raw[:, :, :CAST].rearrange("p j (c i) -> p c j i", i=4),
        )
        q_words = sb.tile([P, Q], U32, name="q_words", align_bytes=64)
        q_scale = sb.tile([P, Q], U8, name="q_scale", align_bytes=64)
        nc.vector.quantize_mx(out=q_words[:].bitcast(FP8X4), scales=q_scale[:], in_=q_bf[:].rearrange("p w j -> p (w j)"))

        a_ps = [ps.tile([P, N], F32, name="a_ps%d" % c) for c in range(T // N)]
        b_ps = [ps.tile([P, N], F32, name="b_ps%d" % c) for c in range(U // N)]
        a = sb.tile([P, T], F32, name="a")
        b = sb.tile([P, U], F32, name="b")
        for c in range(T // N):
            nc.tensor.matmul_mx(
                out=a_ps[c][:], lhsT=q_words[:].bitcast(FP8X4), lhsT_scale=q_scale[:],
                rhs=k_words[:, 2 * N * c : 2 * N * (c + 1)].bitcast(FP4X4), rhs_scale=k_scale[:, N * c : N * (c + 1)],
                start=True, stop=True,
            )
            if c % 2 == 0:
                nc.scalar.copy(out=a[:, N * c : N * (c + 1)], in_=a_ps[c][:])
            else:
                nc.vector.tensor_copy(out=a[:, N * c : N * (c + 1)], in_=a_ps[c][:])
        for c in range(U // N):
            nc.tensor.matmul_mx(
                out=b_ps[c][:], lhsT=q_words[:].bitcast(FP8X4), lhsT_scale=q_scale[:],
                rhs=n_words[:, N * c : N * (c + 1)].bitcast(FP8X4), rhs_scale=n_scale[:, N * c : N * (c + 1)],
                start=True, stop=True,
            )
            if c == U // N - 1:
                nc.scalar.copy(out=b[:, N * c : N * (c + 1)], in_=b_ps[c][:])
            else:
                nc.vector.tensor_copy(out=b[:, N * c : N * (c + 1)], in_=b_ps[c][:])

        h = [slice(0, HALF // 16), slice(HALF // 16, I // 16)]
        got_a = [sb.tile([P, HALF], F32, name="got_a%d" % s) for s in range(2)]
        got_b = sb.tile([P, HALF], F32, name="got_b")
        r = sb.tile([P, I], F32, name="r")
        for s in range(2):
            nc.scalar.activation(got_a[s][:], a[:].indirect(l1[:, h[s]]), COPY)
        nc.vector.tensor_tensor(r[:, :HALF], b[:].indirect(l2[:, h[0]]), got_a[0][:], SUB)
        nc.scalar.activation(got_b[:], b[:].indirect(l2[:, h[1]]), COPY)
        nc.gpsimd.tensor_tensor(r[:, HALF:], got_b[:], got_a[1][:], SUB)

        nc.vector.tensor_copy(f2[:].indirect(l2[:, h[0]]), r[:, :HALF])
        nc.vector.tensor_copy(f2[:].indirect(l2[:, h[1]]), r[:, HALF:])
        b2 = sb.tile([P, U], F32, name="b2")
        nc.gpsimd.tensor_tensor(b2[:], b[:], f2[:], SUB)
        nc.vector.tensor_copy(f1[:].indirect(l1[:]), r[:])
        got_b2 = sb.tile([P, HALF], F32, name="got_b2", tag="late")
        nc.scalar.activation(got_b2[:], b2[:].indirect(l4[:, h[0]]), COPY)
        lam_b2 = sb.tile([P, HALF], F32, name="lam_b2")
        nc.scalar.activation(lam_b2[:], got_b2[:], COPY, scale=lam_col[:])
        neg_b2 = sb.tile([P, HALF], F32, name="neg_b2")
        nc.scalar.activation(neg_b2[:], b2[:].indirect(l4[:, h[1]]), COPY, scale=-1.0)
        a2 = sb.tile([P, T], F32, name="a2")
        nc.gpsimd.tensor_tensor(a2[:, SPLIT:], a[:, SPLIT:], f1[:, SPLIT:], ADD)
        for c0 in range(0, SPLIT, N):
            w = min(N, SPLIT - c0)
            nc.vector.tensor_tensor(a2[:, c0 : c0 + w], a_ps[c0 // N][:, :w], f1[:, c0 : c0 + w], ADD)

        y = [sb.tile([P, HALF], F32, name="y%d" % s) for s in range(2)]
        got_a2 = sb.tile([P, HALF], F32, name="got_a2", tag="late")
        nc.scalar.activation(got_a2[:], a2[:].indirect(l3[:, h[1]]), COPY)
        nc.vector.tensor_tensor(y[0][:], a2[:].indirect(l3[:, h[0]]), lam_b2[:], SUB)
        nc.sync.dma_start(out=out[:, :HALF], in_=y[0][:])
        nc.vector.scalar_tensor_tensor(y[1][:], neg_b2[:], lam_col[:], got_a2[:], MULT, ADD)
        nc.scalar.dma_start(out=out[:, HALF:], in_=y[1][:])
